import numpy as np
import ml_dtypes


def mxq(x, axis, fmt="e4m3"):
    dtype, down = {"e4m3": (ml_dtypes.float8_e4m3fn, 7), "e5m2": (ml_dtypes.float8_e5m2, 14)}[fmt]
    v = np.moveaxis(np.asarray(x, np.float32).astype(ml_dtypes.bfloat16).astype(np.float64), axis, -1)
    blocks = v.reshape(v.shape[:-1] + (-1, 32))
    amax = np.abs(blocks).max(-1, keepdims=True)
    byte = np.maximum(np.where(amax > 0, np.frexp(amax)[1] - 1 + 127, 0) - down, 1)
    scale = np.exp2(byte - 127.0)
    codes = (blocks / scale).astype(np.float32).astype(dtype).astype(np.float64)
    return np.moveaxis((codes * scale).reshape(v.shape), -1, axis)


WIDE = False


def mx_kscale(k):
    if not WIDE:
        return np.ones(k)
    levels = np.array([10, -10, 5, -5, 0])
    if k % 512:
        return np.exp2(np.random.permutation(np.resize(levels, k // 32))).repeat(32)
    a = np.empty((k // 512, 16))
    for p in range(k // 512):
        a[p, :8] = np.random.permutation(np.resize(levels, 8))
        for g in range(8):
            far = levels[np.abs(levels - a[p, g]) >= 10]
            a[p, g + 8] = far[np.random.randint(len(far))]
    return np.exp2(a.ravel()).repeat(32)


def f64(x):
    return np.asarray(x).astype(np.float64)


def striped(idx):
    return np.tile(idx.reshape(-1, 16).T, (8, 1)).astype(np.uint16)


def unstriped(offs):
    return offs[:16].T.reshape(-1).astype(np.int64)


def striped8(idx):
    return np.concatenate([x.reshape(-1, 16).T for x in idx]).astype(np.uint16)


def runs(offs, k):
    lists = np.stack([offs[16 * r : 16 * r + 16].T.reshape(-1) for r in range(8)]).astype(np.int64)
    return lists[np.arange(k) % 512 // 64]


def pack_weight(w):
    k, n = w.shape
    w = f64(np.asarray(w, np.float32).astype(ml_dtypes.bfloat16)).reshape(k // 32, 32, n)
    amax = np.abs(w).max(1)
    byte = np.clip(np.where(amax > 0, np.frexp(amax)[1] - 1 + 127 - 7, 1), 1, 254)
    scaled = (w * np.exp2(127.0 - byte)[:, None, :]).reshape(k, n).astype(np.float32)
    words = np.ascontiguousarray(scaled.reshape(k // 512, 128, 4, n).transpose(0, 1, 3, 2)).astype(ml_dtypes.float8_e4m3fn).view(np.uint8)
    return words, np.ascontiguousarray(byte.astype(np.uint8).reshape(k // 512, 16, n))


def unpack_weight(words, scales):
    g, p, n, _ = words.shape
    vals = np.ascontiguousarray(words).view(ml_dtypes.float8_e4m3fn).astype(np.float64) * np.repeat(np.exp2(scales.astype(np.float64) - 127.0), 8, axis=1)[..., None]
    return vals.transpose(0, 1, 3, 2).reshape(g * 512, n)


def relu(v):
    return np.maximum(v, 0.0)


K, T, S, U, G, H = 512, 2048, 512, 1024, 2048, 512


def setup_inputs():
    n = np.random.standard_normal
    s = mx_kscale(K)[:, None]
    packed_xT = pack_weight(n((K, T)) * s)
    packed_dT = pack_weight(n((K, G)) / s)
    return {
        "x_words": packed_xT[0],
        "x_scales": packed_xT[1],
        "d_words": packed_dT[0],
        "d_scales": packed_dT[1],
        "mem": n((H, U)).astype(np.float32),
        "gs": (np.random.uniform(0.5, 1.5, (K, 1)) * s).astype(np.float32),
        "offs": striped(np.random.permutation(T)[:S]),
        "k1": striped8(np.random.randint(0, G, (8, H))),
        "slot": striped8(np.stack([np.random.permutation(U)[:S] for _ in range(8)])),
        "k2": striped8(np.random.randint(0, G, (8, H))),
    }


def reference(x_words, x_scales, d_words, d_scales, mem, gs, offs, k1, slot, k2):
    d_k2 = unpack_weight(d_words, d_scales)[np.arange(K)[:, None], runs(k2, K)]
    d_k1 = unpack_weight(d_words, d_scales)[np.arange(K)[:, None], runs(k1, K)]
    xq = unpack_weight(x_words, x_scales)[:, unstriped(offs)]
    h = relu(0.0625 * (d_k1.T @ xq))
    pg = f64(mem).copy()
    pg[np.arange(H)[:, None], runs(slot, H)] = h
    z = f64(gs) * pg
    return 0.0625 * ((d_k2.T @ mxq(z, 0, "e4m3")))

@@ -1,0 +1,175 @@
+from contextlib import ExitStack
+
+import concourse.mybir as mybir
+
+K, T, S, U, G, H = 512, 2048, 512, 1024, 2048, 512
+FLOPS = 2 * K * H * S + 2 * K * H * U
+
+F32 = mybir.dt.float32
+BF16 = mybir.dt.bfloat16
+I32 = mybir.dt.int32
+U32 = mybir.dt.uint32
+U16 = mybir.dt.uint16
+U8 = mybir.dt.uint8
+FP8X4 = mybir.dt.float8_e4m3fn_x4
+RELU = mybir.ActivationFunctionType.Relu
+COPY = mybir.ActivationFunctionType.Copy
+MULT = mybir.AluOpType.mult
+
+P = 128
+PACK = 4
+CHUNK = 256
+HALF = S // 2
+SIXTEENTH = 0.0625
+PLANE_ORDER = (2, 0, 1, 3)
+VECTOR_BANKS = 2
+
+
+def tile_picked_pqscat_relu_p_kernel(tc, x_words, x_scales, d_words, d_scales, mem, gs, offs, k1, slot, k2, out):
+    nc = tc.nc
+    with ExitStack() as ctx:
+        lists = ctx.enter_context(tc.tile_pool(name="lists", bufs=1))
+        keep = ctx.enter_context(tc.tile_pool(name="keep", bufs=1))
+        psum = ctx.enter_context(tc.psum_pool(name="psum", bufs=8))
+
+        k1_t = lists.tile([P, H // 16], U16, name="k1_t")
+        offs_t = lists.tile([P, S // 16], U16, name="offs_t")
+        k2_t = lists.tile([P, H // 16], U16, name="k2_t")
+        slot_t = lists.tile([P, S // 16], U16, name="slot_t")
+
+        d_scale_tab = keep.tile([P, G], U8, name="d_scale_tab", tag="shared1", align_bytes=64)
+        x_scale_tab = keep.tile([P, T], U8, name="x_scale_tab", align_bytes=64)
+        d_word_tab = keep.tile([P, G], I32, name="d_word_tab", tag="shared3", align_bytes=64)
+        x_word_tab = keep.tile([P, T], I32, name="x_word_tab", tag="shared2", align_bytes=64)
+
+        nc.sync.dma_start(k1_t[:], k1)
+        nc.sync.dma_start(d_scale_tab[:].bitcast(I32), d_scales[0].bitcast(I32).unsqueeze(1).to_broadcast([16, 8, G // 4]))
+        nc.sync.dma_start(offs_t[:], offs)
+        nc.sync.dma_start(x_scale_tab[:].bitcast(I32), x_scales[0].bitcast(I32).unsqueeze(1).to_broadcast([16, 8, T // 4]))
+        nc.sync.dma_start(k2_t[:], k2)
+        nc.sync.dma_start(d_word_tab[:], d_words[0].rearrange("p c r -> p (c r)").bitcast(I32))
+        nc.sync.dma_start(x_word_tab[:], x_words[0].rearrange("p c r -> p (c r)").bitcast(I32))
+        nc.sync.dma_start(slot_t[:], slot)
+        gain = keep.tile([P, PACK], F32, name="gain")
+        nc.sync.dma_start(gain[:], gs.rearrange("(p t) o -> p (t o)", t=PACK))
+
+        k1_bytes = keep.tile([P, H], U8, name="k1_bytes", align_bytes=64)
+        x_bytes = keep.tile([P, S], U8, name="x_bytes", tag="shared0", align_bytes=64)
+        k2_bytes = keep.tile([P, H], U8, name="k2_bytes", align_bytes=64)
+        staged = keep.tile([P, H + S], U8, name="staged", align_bytes=64)
+        planes = keep.tile([P, H + S], U8, name="planes", align_bytes=64)
+        w2_scales = keep.tile([P, H], U8, name="w2_scales", align_bytes=64)
+        nc.vector.memset(planes[:].bitcast(I32), 0)
+        nc.vector.memset(w2_scales[:].bitcast(I32), 0)
+
+        def place_scale_rows(queue, plane, picked):
+            for q in range(4):
+                queue.dma_start(plane[32 * q : 32 * q + 4, :].bitcast(I32), picked[32 * q : 32 * q + 32 : 8, :].bitcast(I32))
+
+        nc.vector.tensor_copy(k1_bytes[:], d_scale_tab[:].indirect(k1_t[:]))
+        nc.vector.tensor_copy(x_bytes[:], x_scale_tab[:].indirect(offs_t[:]))
+        nc.vector.tensor_copy(
+            staged[:, 0:H].rearrange("p (t m) -> p t m", t=PACK),
+            k1_bytes[:].rearrange("p (m t) -> p t m", t=PACK),
+        )
+        nc.vector.tensor_copy(staged[:, H:].bitcast(I32), x_bytes[:].bitcast(I32))
+        place_scale_rows(nc.scalar, planes, staged)
+        w1_scales = planes[:, 0:H]
+        x_sel_scales = planes[:, H : H + S]
+
+        k1_words = keep.tile([P, H], U32, name="k1_words", align_bytes=64)
+        w1 = keep.tile([P, H], U32, name="w1", align_bytes=64)
+        x_sel = keep.tile([P, S], U32, name="x_sel", align_bytes=64)
+        w2 = keep.tile([P, H], U32, name="w2", align_bytes=64)
+        nc.vector.tensor_copy(k1_words[:], d_word_tab[:].bitcast(U32).indirect(k1_t[:]))
+        nc.vector.tensor_copy(k2_bytes[:], d_scale_tab[:].indirect(k2_t[:]))
+        nc.vector.tensor_copy(
+            w1[:].rearrange("p (t m) -> p t m", t=PACK),
+            k1_words[:].rearrange("p (m t) -> p t m", t=PACK),
+        )
+        for half in range(2):
+            nc.vector.tensor_copy(
+                x_sel[:, half * HALF : (half + 1) * HALF],
+                x_word_tab[:].bitcast(U32).indirect(offs_t[:, half * HALF // 16 : (half + 1) * HALF // 16]),
+            )
+        nc.vector.tensor_copy(w2[:], d_word_tab[:].bitcast(U32).indirect(k2_t[:]))
+        place_scale_rows(nc.sync, w2_scales, k2_bytes)
+
+        mem_rows = mem.rearrange("(p t) w -> p t w", t=PACK)
+        n_chunks = U // CHUNK
+        z = [keep.tile([P, CHUNK, PACK], BF16, name="z%d" % c, align_bytes=64) for c in range(n_chunks)]
+        pages = {}
+        for n, t in enumerate(PLANE_ORDER):
+            pages[t] = keep.tile([P, U], F32, name="page%d" % t, tag="shared%d" % n, align_bytes=64)
+            nc.sync.dma_start(pages[t][:], mem_rows[:, t, :])
+
+        def first_layer(t, h, tokens):
+            acc = psum.tile([P, tokens.stop - tokens.start], F32, name="acc", tag="bank")
+            cols = slice(P * t, P * (t + 1))
+            nc.tensor.matmul_mx(
+                out=acc[:],
+                lhsT=w1[:, cols].bitcast(FP8X4),
+                lhsT_scale=w1_scales[:, cols],
+                rhs=x_sel[:, tokens].bitcast(FP8X4),
+                rhs_scale=x_sel_scales[:, tokens],
+                start=True,
+                stop=True,
+            )
+            nc.scalar.activation(h[:], acc[:], RELU, scale=SIXTEENTH)
+
+        def weigh_on_scalar(t):
+            for c in range(n_chunks):
+                nc.scalar.activation(z[c][:, :, t], pages[t][:, c * CHUNK : (c + 1) * CHUNK], COPY, scale=gain[:, t : t + 1])
+
+        first, last = PLANE_ORDER[0], PLANE_ORDER[-1]
+        h_first = [keep.tile([P, HALF], F32, name="h_first%d" % half) for half in range(2)]
+        for half in range(2):
+            first_layer(first, h_first[half], slice(half * HALF, (half + 1) * HALF))
+        hs = {}
+        for t in PLANE_ORDER[1:-1]:
+            hs[t] = keep.tile([P, S], F32, name="h%d" % t)
+            first_layer(t, hs[t], slice(0, S))
+        for half in range(2):
+            nc.vector.tensor_copy(pages[first][:].indirect(slot_t[:, half * HALF // 16 : (half + 1) * HALF // 16]), h_first[half][:])
+        weigh_on_scalar(first)
+        hs[last] = keep.tile([P, S], F32, name="h_last", tag="shared0", align_bytes=64)
+        first_layer(last, hs[last], slice(0, S))
+        for t in PLANE_ORDER[1:-1]:
+            nc.vector.tensor_copy(pages[t][:].indirect(slot_t[:]), hs[t][:])
+            weigh_on_scalar(t)
+        nc.vector.tensor_copy(pages[last][:].indirect(slot_t[:]), hs[last][:])
+
+        codes = [keep.tile([P, CHUNK], U32, name="codes%d" % c, align_bytes=64) for c in range(n_chunks)]
+        z_scales = [keep.tile([P, CHUNK], U8, name="z_scales%d" % c, align_bytes=64) for c in range(n_chunks)]
+        out_rows = out.rearrange("(m p) w -> p m w", p=P)
+
+        def weigh_last(c):
+            nc.vector.tensor_scalar(z[c][:, :, last], pages[last][:, c * CHUNK : (c + 1) * CHUNK], gain[:, last : last + 1], None, MULT)
+
+        def second_layer(c):
+            nc.vector.quantize_mx(codes[c][:].bitcast(FP8X4), z_scales[c][:], z[c][:].rearrange("p w t -> p (w t)"))
+            for half in range(2):
+                acc = psum.tile([P, 2, CHUNK], F32, name="acc2", tag="bank")
+                for i in range(2):
+                    cols = slice(P * (2 * half + i), P * (2 * half + i + 1))
+                    nc.tensor.matmul_mx(
+                        out=acc[:, i, :],
+                        lhsT=w2[:, cols].bitcast(FP8X4),
+                        lhsT_scale=w2_scales[:, cols],
+                        rhs=codes[c][:].bitcast(FP8X4),
+                        rhs_scale=z_scales[c][:],
+                        start=True,
+                        stop=True,
+                    )
+                res = keep.tile([P, 2, CHUNK], F32, name="res%d_%d" % (c, half))
+                if 2 * c + half >= 2 * n_chunks - 2 * VECTOR_BANKS and half == 1:
+                    nc.vector.tensor_scalar(res[:], acc[:], SIXTEENTH, None, MULT)
+                else:
+                    nc.scalar.activation(res[:], acc[:], COPY, scale=SIXTEENTH)
+                nc.sync.dma_start(out_rows[:, 2 * half : 2 * half + 2, c * CHUNK : (c + 1) * CHUNK], res[:])
+
+        weigh_last(0)
+        for c in range(n_chunks):
+            if c + 1 < n_chunks:
+                weigh_last(c + 1)
+            second_layer(c)

@@ -22,7 +22,6 @@ CHUNK = 256
 HALF = S // 2
 SIXTEENTH = 0.0625
 PLANE_ORDER = (2, 0, 1, 3)
-VECTOR_BANKS = 2
 
 
 def tile_picked_pqscat_relu_p_kernel(tc, x_words, x_scales, d_words, d_scales, mem, gs, offs, k1, slot, k2, out):
@@ -37,11 +36,16 @@ def tile_picked_pqscat_relu_p_kernel(tc, x_words, x_scales, d_words, d_scales, m
         k2_t = lists.tile([P, H // 16], U16, name="k2_t")
         slot_t = lists.tile([P, S // 16], U16, name="slot_t")
 
-        d_scale_tab = keep.tile([P, G], U8, name="d_scale_tab", tag="shared1", align_bytes=64)
+        d_scale_tab = keep.tile([P, G], U8, name="d_scale_tab", align_bytes=64)
         x_scale_tab = keep.tile([P, T], U8, name="x_scale_tab", align_bytes=64)
-        d_word_tab = keep.tile([P, G], I32, name="d_word_tab", tag="shared3", align_bytes=64)
-        x_word_tab = keep.tile([P, T], I32, name="x_word_tab", tag="shared2", align_bytes=64)
+        d_word_tab = keep.tile([P, G], I32, name="d_word_tab", tag="page1", align_bytes=64)
+        x_word_tab = keep.tile([P, T], I32, name="x_word_tab", tag="w2", align_bytes=64)
+        placed = keep.tile([P, H + S], U8, name="placed", align_bytes=64)
+        w2_scales = keep.tile([P, H], U8, name="w2_scales", align_bytes=64)
+        gain = keep.tile([P, PACK], F32, name="gain")
 
+        nc.vector.memset(placed[:].bitcast(I32), 0)
+        nc.vector.memset(w2_scales[:].bitcast(I32), 0)
         nc.sync.dma_start(k1_t[:], k1)
         nc.sync.dma_start(d_scale_tab[:].bitcast(I32), d_scales[0].bitcast(I32).unsqueeze(1).to_broadcast([16, 8, G // 4]))
         nc.sync.dma_start(offs_t[:], offs)
@@ -49,127 +53,151 @@ def tile_picked_pqscat_relu_p_kernel(tc, x_words, x_scales, d_words, d_scales, m
         nc.sync.dma_start(k2_t[:], k2)
         nc.sync.dma_start(d_word_tab[:], d_words[0].rearrange("p c r -> p (c r)").bitcast(I32))
         nc.sync.dma_start(x_word_tab[:], x_words[0].rearrange("p c r -> p (c r)").bitcast(I32))
+        mem_rows = mem.rearrange("(p t) w -> p t w", t=PACK)
+        first, last = PLANE_ORDER[0], PLANE_ORDER[-1]
+        pages = {first: keep.tile([P, U], F32, name="page_first", tag="page0", align_bytes=64)}
+        nc.sync.dma_start(pages[first][:], mem_rows[:, first, :])
         nc.sync.dma_start(slot_t[:], slot)
-        gain = keep.tile([P, PACK], F32, name="gain")
         nc.sync.dma_start(gain[:], gs.rearrange("(p t) o -> p (t o)", t=PACK))
-
-        k1_bytes = keep.tile([P, H], U8, name="k1_bytes", align_bytes=64)
-        x_bytes = keep.tile([P, S], U8, name="x_bytes", tag="shared0", align_bytes=64)
-        k2_bytes = keep.tile([P, H], U8, name="k2_bytes", align_bytes=64)
-        staged = keep.tile([P, H + S], U8, name="staged", align_bytes=64)
-        planes = keep.tile([P, H + S], U8, name="planes", align_bytes=64)
-        w2_scales = keep.tile([P, H], U8, name="w2_scales", align_bytes=64)
-        nc.vector.memset(planes[:].bitcast(I32), 0)
-        nc.vector.memset(w2_scales[:].bitcast(I32), 0)
 
         def place_scale_rows(queue, plane, picked):
             for q in range(4):
                 queue.dma_start(plane[32 * q : 32 * q + 4, :].bitcast(I32), picked[32 * q : 32 * q + 32 : 8, :].bitcast(I32))
 
-        nc.vector.tensor_copy(k1_bytes[:], d_scale_tab[:].indirect(k1_t[:]))
-        nc.vector.tensor_copy(x_bytes[:], x_scale_tab[:].indirect(offs_t[:]))
-        nc.vector.tensor_copy(
-            staged[:, 0:H].rearrange("p (t m) -> p t m", t=PACK),
-            k1_bytes[:].rearrange("p (m t) -> p t m", t=PACK),
-        )
-        nc.vector.tensor_copy(staged[:, H:].bitcast(I32), x_bytes[:].bitcast(I32))
-        place_scale_rows(nc.scalar, planes, staged)
-        w1_scales = planes[:, 0:H]
-        x_sel_scales = planes[:, H : H + S]
+        first_bytes = keep.tile([P, H + S], U8, name="first_bytes", align_bytes=64)
+        k2_bytes = keep.tile([P, H], U8, name="k2_bytes", align_bytes=64)
+        nc.vector.tensor_copy(first_bytes[:, 0:H], d_scale_tab[:].indirect(k1_t[:]))
+        nc.vector.tensor_copy(first_bytes[:, H:], x_scale_tab[:].indirect(offs_t[:]))
+        place_scale_rows(nc.scalar, placed, first_bytes)
+        nc.vector.tensor_copy(k2_bytes[:], d_scale_tab[:].indirect(k2_t[:]))
+        place_scale_rows(nc.sync, w2_scales, k2_bytes)
+        x_sel_scales = placed[:, H:]
 
         k1_words = keep.tile([P, H], U32, name="k1_words", align_bytes=64)
         w1 = keep.tile([P, H], U32, name="w1", align_bytes=64)
-        x_sel = keep.tile([P, S], U32, name="x_sel", align_bytes=64)
-        w2 = keep.tile([P, H], U32, name="w2", align_bytes=64)
+        w1_scales = keep.tile([P, H], U8, name="w1_scales", align_bytes=64)
+        x_sel = [keep.tile([P, HALF], U32, name="x_sel%d" % half, tag="page%d" % (2 + half), align_bytes=64) for half in range(2)]
+
+        def pick_tokens(half):
+            nc.vector.tensor_copy(
+                x_sel[half][:],
+                x_word_tab[:].bitcast(U32).indirect(offs_t[:, half * HALF // 16 : (half + 1) * HALF // 16]),
+            )
+
         nc.vector.tensor_copy(k1_words[:], d_word_tab[:].bitcast(U32).indirect(k1_t[:]))
-        nc.vector.tensor_copy(k2_bytes[:], d_scale_tab[:].indirect(k2_t[:]))
         nc.vector.tensor_copy(
             w1[:].rearrange("p (t m) -> p t m", t=PACK),
             k1_words[:].rearrange("p (m t) -> p t m", t=PACK),
         )
-        for half in range(2):
-            nc.vector.tensor_copy(
-                x_sel[:, half * HALF : (half + 1) * HALF],
-                x_word_tab[:].bitcast(U32).indirect(offs_t[:, half * HALF // 16 : (half + 1) * HALF // 16]),
-            )
+        pick_tokens(0)
+        nc.vector.tensor_copy(
+            w1_scales[:].rearrange("p (t m) -> p t m", t=PACK),
+            placed[:, 0:H].rearrange("p (m t) -> p t m", t=PACK),
+        )
+        pick_tokens(1)
+        w2 = keep.tile([P, H], U32, name="w2", tag="w2", align_bytes=64)
         nc.vector.tensor_copy(w2[:], d_word_tab[:].bitcast(U32).indirect(k2_t[:]))
-        place_scale_rows(nc.sync, w2_scales, k2_bytes)
 
-        mem_rows = mem.rearrange("(p t) w -> p t w", t=PACK)
-        n_chunks = U // CHUNK
-        z = [keep.tile([P, CHUNK, PACK], BF16, name="z%d" % c, align_bytes=64) for c in range(n_chunks)]
-        pages = {}
-        for n, t in enumerate(PLANE_ORDER):
-            pages[t] = keep.tile([P, U], F32, name="page%d" % t, tag="shared%d" % n, align_bytes=64)
+        for n in range(1, PACK):
+            t = PLANE_ORDER[n]
+            pages[t] = keep.tile([P, U], F32, name="page%d" % t, tag="page%d" % n, align_bytes=64)
             nc.sync.dma_start(pages[t][:], mem_rows[:, t, :])
 
-        def first_layer(t, h, tokens):
-            acc = psum.tile([P, tokens.stop - tokens.start], F32, name="acc", tag="bank")
+        def first_layer(t, h, halves):
+            acc = psum.tile([P, len(halves), HALF], F32, name="acc", tag="bank")
             cols = slice(P * t, P * (t + 1))
-            nc.tensor.matmul_mx(
-                out=acc[:],
-                lhsT=w1[:, cols].bitcast(FP8X4),
-                lhsT_scale=w1_scales[:, cols],
-                rhs=x_sel[:, tokens].bitcast(FP8X4),
-                rhs_scale=x_sel_scales[:, tokens],
-                start=True,
-                stop=True,
-            )
-            nc.scalar.activation(h[:], acc[:], RELU, scale=SIXTEENTH)
+            for i, half in enumerate(halves):
+                nc.tensor.matmul_mx(
+                    out=acc[:, i, :],
+                    lhsT=w1[:, cols].bitcast(FP8X4),
+                    lhsT_scale=w1_scales[:, cols],
+                    rhs=x_sel[half][:].bitcast(FP8X4),
+                    rhs_scale=x_sel_scales[:, half * HALF : (half + 1) * HALF],
+                    start=True,
+                    stop=True,
+                )
+            nc.scalar.activation(h[:], acc[:].rearrange("p i s -> p (i s)"), RELU, scale=SIXTEENTH)
 
-        def weigh_on_scalar(t):
-            for c in range(n_chunks):
-                nc.scalar.activation(z[c][:, :, t], pages[t][:, c * CHUNK : (c + 1) * CHUNK], COPY, scale=gain[:, t : t + 1])
-
-        first, last = PLANE_ORDER[0], PLANE_ORDER[-1]
         h_first = [keep.tile([P, HALF], F32, name="h_first%d" % half) for half in range(2)]
         for half in range(2):
-            first_layer(first, h_first[half], slice(half * HALF, (half + 1) * HALF))
+            first_layer(first, h_first[half], (half,))
         hs = {}
         for t in PLANE_ORDER[1:-1]:
             hs[t] = keep.tile([P, S], F32, name="h%d" % t)
-            first_layer(t, hs[t], slice(0, S))
+            first_layer(t, hs[t], (0, 1))
+
+        n_chunks = U // CHUNK
+        z = [keep.tile([P, CHUNK, PACK], BF16, name="z%d" % c, align_bytes=64) for c in range(n_chunks)]
+        late = {c: keep.tile([P, 2, CHUNK], BF16, name="late%d" % c, align_bytes=64) for c in range(1, n_chunks)}
+
+        def page_chunk(t, c):
+            return pages[t][:, c * CHUNK : (c + 1) * CHUNK]
+
+        def weigh(t, chunks):
+            for c in chunks:
+                target = late[c][:, t - 2, :] if t >= 2 and c in late else z[c][:, :, t]
+                nc.scalar.activation(target, page_chunk(t, c), COPY, scale=gain[:, t : t + 1])
+
         for half in range(2):
-            nc.vector.tensor_copy(pages[first][:].indirect(slot_t[:, half * HALF // 16 : (half + 1) * HALF // 16]), h_first[half][:])
-        weigh_on_scalar(first)
-        hs[last] = keep.tile([P, S], F32, name="h_last", tag="shared0", align_bytes=64)
-        first_layer(last, hs[last], slice(0, S))
+            offsets = slot_t[:, half * HALF // 16 : (half + 1) * HALF // 16]
+            nc.vector.tensor_copy(pages[first][:].indirect(offsets), h_first[half][:])
+        weigh(first, range(n_chunks))
+        hs[last] = keep.tile([P, S], F32, name="h_last", tag="page0", align_bytes=64)
+        first_layer(last, hs[last], (0, 1))
         for t in PLANE_ORDER[1:-1]:
             nc.vector.tensor_copy(pages[t][:].indirect(slot_t[:]), hs[t][:])
-            weigh_on_scalar(t)
+            weigh(t, range(n_chunks))
         nc.vector.tensor_copy(pages[last][:].indirect(slot_t[:]), hs[last][:])
+        nc.vector.tensor_scalar(z[0][:, :, last], page_chunk(last, 0), gain[:, last : last + 1], None, MULT)
+        weigh(last, range(1, n_chunks))
 
-        codes = [keep.tile([P, CHUNK], U32, name="codes%d" % c, align_bytes=64) for c in range(n_chunks)]
-        z_scales = [keep.tile([P, CHUNK], U8, name="z_scales%d" % c, align_bytes=64) for c in range(n_chunks)]
         out_rows = out.rearrange("(m p) w -> p m w", p=P)
+        spans = ((0, 1), (1, 2), (2, 4))
+        codes, z_scales, home = {}, {}, {}
+        for c0, c1 in spans:
+            codes[c0] = keep.tile([P, (c1 - c0) * CHUNK], U32, name="codes%d" % c0, align_bytes=64)
+            z_scales[c0] = keep.tile([P, (c1 - c0) * CHUNK], U8, name="z_scales%d" % c0, align_bytes=64)
+            for c in range(c0, c1):
+                home[c] = (c0, slice((c - c0) * CHUNK, (c - c0 + 1) * CHUNK))
 
-        def weigh_last(c):
-            nc.vector.tensor_scalar(z[c][:, :, last], pages[last][:, c * CHUNK : (c + 1) * CHUNK], gain[:, last : last + 1], None, MULT)
+        def pair(c):
+            nc.vector.tensor_copy(z[c][:, :, 2:4], late[c][:].rearrange("p t w -> p w t"))
 
-        def second_layer(c):
-            nc.vector.quantize_mx(codes[c][:].bitcast(FP8X4), z_scales[c][:], z[c][:].rearrange("p w t -> p (w t)"))
-            for half in range(2):
-                acc = psum.tile([P, 2, CHUNK], F32, name="acc2", tag="bank")
-                for i in range(2):
-                    cols = slice(P * (2 * half + i), P * (2 * half + i + 1))
-                    nc.tensor.matmul_mx(
-                        out=acc[:, i, :],
-                        lhsT=w2[:, cols].bitcast(FP8X4),
-                        lhsT_scale=w2_scales[:, cols],
-                        rhs=codes[c][:].bitcast(FP8X4),
-                        rhs_scale=z_scales[c][:],
-                        start=True,
-                        stop=True,
-                    )
-                res = keep.tile([P, 2, CHUNK], F32, name="res%d_%d" % (c, half))
-                if 2 * c + half >= 2 * n_chunks - 2 * VECTOR_BANKS and half == 1:
-                    nc.vector.tensor_scalar(res[:], acc[:], SIXTEENTH, None, MULT)
-                else:
-                    nc.scalar.activation(res[:], acc[:], COPY, scale=SIXTEENTH)
-                nc.sync.dma_start(out_rows[:, 2 * half : 2 * half + 2, c * CHUNK : (c + 1) * CHUNK], res[:])
+        def quantize(c):
+            c0, cols = home[c]
+            nc.vector.quantize_mx(codes[c0][:, cols].bitcast(FP8X4), z_scales[c0][:, cols], z[c][:].rearrange("p w t -> p (w t)"))
 
-        weigh_last(0)
-        for c in range(n_chunks):
-            if c + 1 < n_chunks:
-                weigh_last(c + 1)
-            second_layer(c)
+        def second_layer(c0, c1, blocks, on_vector):
+            width = (c1 - c0) * CHUNK
+            acc = psum.tile([P, len(blocks), width], F32, name="acc2", tag="bank")
+            for i, m in enumerate(blocks):
+                cols = slice(P * m, P * (m + 1))
+                nc.tensor.matmul_mx(
+                    out=acc[:, i, :],
+                    lhsT=w2[:, cols].bitcast(FP8X4),
+                    lhsT_scale=w2_scales[:, cols],
+                    rhs=codes[c0][:].bitcast(FP8X4),
+                    rhs_scale=z_scales[c0][:],
+                    start=True,
+                    stop=True,
+                )
+            res = keep.tile([P, len(blocks), width], F32, name="res%d_%d" % (c0, blocks[0]))
+            if on_vector:
+                nc.vector.tensor_scalar(res[:], acc[:], SIXTEENTH, None, MULT)
+            else:
+                nc.scalar.activation(res[:], acc[:], COPY, scale=SIXTEENTH)
+            nc.sync.dma_start(out_rows[:, blocks[0] : blocks[-1] + 1, c0 * CHUNK : c1 * CHUNK], res[:])
+
+        quantize(0)
+        for blocks in ((0,), (1,), (2, 3)):
+            second_layer(0, 1, blocks, False)
+        pair(1)
+        pair(2)
+        quantize(1)
+        for blocks in ((0, 1), (2, 3)):
+            second_layer(1, 2, blocks, False)
+        pair(3)
+        quantize(2)
+        quantize(3)
+        for m in range(H // P):
+            second_layer(2, 4, (m,), m % 2 == 1)

@@ -36,16 +36,14 @@ def tile_picked_pqscat_relu_p_kernel(tc, x_words, x_scales, d_words, d_scales, m
         k2_t = lists.tile([P, H // 16], U16, name="k2_t")
         slot_t = lists.tile([P, S // 16], U16, name="slot_t")
 
-        d_scale_tab = keep.tile([P, G], U8, name="d_scale_tab", align_bytes=64)
+        d_scale_tab = keep.tile([P, G], U8, name="d_scale_tab", tag="page0", align_bytes=64)
         x_scale_tab = keep.tile([P, T], U8, name="x_scale_tab", align_bytes=64)
         d_word_tab = keep.tile([P, G], I32, name="d_word_tab", tag="page1", align_bytes=64)
         x_word_tab = keep.tile([P, T], I32, name="x_word_tab", tag="w2", align_bytes=64)
         placed = keep.tile([P, H + S], U8, name="placed", align_bytes=64)
-        w2_scales = keep.tile([P, H], U8, name="w2_scales", align_bytes=64)
         gain = keep.tile([P, PACK], F32, name="gain")
 
         nc.vector.memset(placed[:].bitcast(I32), 0)
-        nc.vector.memset(w2_scales[:].bitcast(I32), 0)
         nc.sync.dma_start(k1_t[:], k1)
         nc.sync.dma_start(d_scale_tab[:].bitcast(I32), d_scales[0].bitcast(I32).unsqueeze(1).to_broadcast([16, 8, G // 4]))
         nc.sync.dma_start(offs_t[:], offs)
@@ -55,22 +53,21 @@ def tile_picked_pqscat_relu_p_kernel(tc, x_words, x_scales, d_words, d_scales, m
         nc.sync.dma_start(x_word_tab[:], x_words[0].rearrange("p c r -> p (c r)").bitcast(I32))
         mem_rows = mem.rearrange("(p t) w -> p t w", t=PACK)
         first, last = PLANE_ORDER[0], PLANE_ORDER[-1]
-        pages = {first: keep.tile([P, U], F32, name="page_first", tag="page0", align_bytes=64)}
-        nc.sync.dma_start(pages[first][:], mem_rows[:, first, :])
+        pages = {}
         nc.sync.dma_start(slot_t[:], slot)
         nc.sync.dma_start(gain[:], gs.rearrange("(p t) o -> p (t o)", t=PACK))
 
-        def place_scale_rows(queue, plane, picked):
+        def place_scale_rows(queue, row0, picked):
+            width = picked.shape[1]
             for q in range(4):
-                queue.dma_start(plane[32 * q : 32 * q + 4, :].bitcast(I32), picked[32 * q : 32 * q + 32 : 8, :].bitcast(I32))
+                queue.dma_start(placed[32 * q + row0 : 32 * q + row0 + 4, 0:width].bitcast(I32), picked[32 * q : 32 * q + 32 : 8, :].bitcast(I32))
 
-        first_bytes = keep.tile([P, H + S], U8, name="first_bytes", align_bytes=64)
+        first_bytes = keep.tile([P, H + S], U8, name="first_bytes", tag="page3", align_bytes=64)
         k2_bytes = keep.tile([P, H], U8, name="k2_bytes", align_bytes=64)
         nc.vector.tensor_copy(first_bytes[:, 0:H], d_scale_tab[:].indirect(k1_t[:]))
         nc.vector.tensor_copy(first_bytes[:, H:], x_scale_tab[:].indirect(offs_t[:]))
-        place_scale_rows(nc.scalar, placed, first_bytes)
+        place_scale_rows(nc.scalar, 0, first_bytes)
         nc.vector.tensor_copy(k2_bytes[:], d_scale_tab[:].indirect(k2_t[:]))
-        place_scale_rows(nc.sync, w2_scales, k2_bytes)
         x_sel_scales = placed[:, H:]
 
         k1_words = keep.tile([P, H], U32, name="k1_words", align_bytes=64)
@@ -94,12 +91,12 @@ def tile_picked_pqscat_relu_p_kernel(tc, x_words, x_scales, d_words, d_scales, m
             w1_scales[:].rearrange("p (t m) -> p t m", t=PACK),
             placed[:, 0:H].rearrange("p (m t) -> p t m", t=PACK),
         )
+        place_scale_rows(nc.sync, 4, k2_bytes)
         pick_tokens(1)
         w2 = keep.tile([P, H], U32, name="w2", tag="w2", align_bytes=64)
         nc.vector.tensor_copy(w2[:], d_word_tab[:].bitcast(U32).indirect(k2_t[:]))
 
-        for n in range(1, PACK):
-            t = PLANE_ORDER[n]
+        for n, t in enumerate(PLANE_ORDER):
             pages[t] = keep.tile([P, U], F32, name="page%d" % t, tag="page%d" % n, align_bytes=64)
             nc.sync.dma_start(pages[t][:], mem_rows[:, t, :])
 
@@ -175,7 +172,7 @@ def tile_picked_pqscat_relu_p_kernel(tc, x_words, x_scales, d_words, d_scales, m
                 nc.tensor.matmul_mx(
                     out=acc[:, i, :],
                     lhsT=w2[:, cols].bitcast(FP8X4),
-                    lhsT_scale=w2_scales[:, cols],
+                    lhsT_scale=placed[4:P, cols],
                     rhs=codes[c0][:].bitcast(FP8X4),
                     rhs_scale=z_scales[c0][:],
                     start=True,

@@ -18,183 +18,187 @@ MULT = mybir.AluOpType.mult
 
 P = 128
 PACK = 4
-CHUNK = 256
-HALF = S // 2
+GROUP = 16
+BLOCK_P = 8
+QUAD = 32
+W2_ROW0 = 4
+HALF = 256
+WORD_BYTES = 4
+BANKS = 8
 SIXTEENTH = 0.0625
-PLANE_ORDER = (2, 0, 1, 3)
+
+PLANE_ORDER = (0, 2, 3, 1)
+WIDTHS = (128, 128, 256, 256, 256)
+DIRECT = 2
+BLOCKS_PER_HALF = HALF // P
 
 
 def tile_picked_pqscat_relu_p_kernel(tc, x_words, x_scales, d_words, d_scales, mem, gs, offs, k1, slot, k2, out):
     nc = tc.nc
+    first, last = PLANE_ORDER[0], PLANE_ORDER[-1]
     with ExitStack() as ctx:
         lists = ctx.enter_context(tc.tile_pool(name="lists", bufs=1))
         keep = ctx.enter_context(tc.tile_pool(name="keep", bufs=1))
-        psum = ctx.enter_context(tc.psum_pool(name="psum", bufs=8))
+        psum = ctx.enter_context(tc.psum_pool(name="psum", bufs=BANKS))
 
-        k1_t = lists.tile([P, H // 16], U16, name="k1_t")
-        offs_t = lists.tile([P, S // 16], U16, name="offs_t")
-        k2_t = lists.tile([P, H // 16], U16, name="k2_t")
-        slot_t = lists.tile([P, S // 16], U16, name="slot_t")
-
+        k1_list = lists.tile([P, H // GROUP], U16, name="k1_list")
+        offs_list = lists.tile([P, S // GROUP], U16, name="offs_list")
+        k2_list = lists.tile([P, H // GROUP], U16, name="k2_list")
+        slot_list = lists.tile([P, S // GROUP], U16, name="slot_list")
         d_scale_tab = keep.tile([P, G], U8, name="d_scale_tab", tag="page0", align_bytes=64)
         x_scale_tab = keep.tile([P, T], U8, name="x_scale_tab", align_bytes=64)
         d_word_tab = keep.tile([P, G], I32, name="d_word_tab", tag="page1", align_bytes=64)
-        x_word_tab = keep.tile([P, T], I32, name="x_word_tab", tag="w2", align_bytes=64)
+        x_word_tab = keep.tile([P, T], I32, name="x_word_tab", tag="w2_high", align_bytes=64)
         placed = keep.tile([P, H + S], U8, name="placed", align_bytes=64)
         gain = keep.tile([P, PACK], F32, name="gain")
 
+        def half_of(list_tile, half):
+            return list_tile[:, half * HALF // GROUP : (half + 1) * HALF // GROUP]
+
+        nc.vector.memset(x_scale_tab[:].bitcast(I32), 0)
         nc.vector.memset(placed[:].bitcast(I32), 0)
-        nc.sync.dma_start(k1_t[:], k1)
-        nc.sync.dma_start(d_scale_tab[:].bitcast(I32), d_scales[0].bitcast(I32).unsqueeze(1).to_broadcast([16, 8, G // 4]))
-        nc.sync.dma_start(offs_t[:], offs)
-        nc.sync.dma_start(x_scale_tab[:].bitcast(I32), x_scales[0].bitcast(I32).unsqueeze(1).to_broadcast([16, 8, T // 4]))
-        nc.sync.dma_start(k2_t[:], k2)
+        nc.sync.dma_start(k1_list[:], k1)
+        nc.sync.dma_start(
+            d_scale_tab[:].bitcast(I32),
+            d_scales[0].bitcast(I32).unsqueeze(1).to_broadcast([P // BLOCK_P, BLOCK_P, G // WORD_BYTES]),
+        )
+        nc.sync.dma_start(offs_list[:], offs)
+        nc.sync.dma_start(k2_list[:], k2)
+        nc.sync.dma_start(slot_list[:], slot)
+        nc.sync.dma_start(x_scale_tab[0:P:BLOCK_P, :].bitcast(I32), x_scales[0].bitcast(I32))
         nc.sync.dma_start(d_word_tab[:], d_words[0].rearrange("p c r -> p (c r)").bitcast(I32))
         nc.sync.dma_start(x_word_tab[:], x_words[0].rearrange("p c r -> p (c r)").bitcast(I32))
-        mem_rows = mem.rearrange("(p t) w -> p t w", t=PACK)
-        first, last = PLANE_ORDER[0], PLANE_ORDER[-1]
-        pages = {}
-        nc.sync.dma_start(slot_t[:], slot)
         nc.sync.dma_start(gain[:], gs.rearrange("(p t) o -> p (t o)", t=PACK))
 
         def place_scale_rows(queue, row0, picked):
             width = picked.shape[1]
-            for q in range(4):
-                queue.dma_start(placed[32 * q + row0 : 32 * q + row0 + 4, 0:width].bitcast(I32), picked[32 * q : 32 * q + 32 : 8, :].bitcast(I32))
+            for q in range(P // QUAD):
+                target = placed[QUAD * q + row0 : QUAD * q + row0 + QUAD // BLOCK_P, 0:width]
+                queue.dma_start(target.bitcast(I32), picked[QUAD * q : QUAD * (q + 1) : BLOCK_P, :].bitcast(I32))
 
         first_bytes = keep.tile([P, H + S], U8, name="first_bytes", tag="page3", align_bytes=64)
         k2_bytes = keep.tile([P, H], U8, name="k2_bytes", align_bytes=64)
-        nc.vector.tensor_copy(first_bytes[:, 0:H], d_scale_tab[:].indirect(k1_t[:]))
-        nc.vector.tensor_copy(first_bytes[:, H:], x_scale_tab[:].indirect(offs_t[:]))
+        nc.vector.tensor_copy(first_bytes[:, 0:H], d_scale_tab[:].indirect(k1_list[:]))
+        nc.vector.tensor_copy(first_bytes[:, H:], x_scale_tab[:].indirect(offs_list[:]))
         place_scale_rows(nc.scalar, 0, first_bytes)
-        nc.vector.tensor_copy(k2_bytes[:], d_scale_tab[:].indirect(k2_t[:]))
-        x_sel_scales = placed[:, H:]
+        nc.vector.tensor_copy(k2_bytes[:], d_scale_tab[:].indirect(k2_list[:]))
+
+        def pick_half(name, tag, table, list_tile, half):
+            words = keep.tile([P, HALF], U32, name=name, tag=tag, align_bytes=64)
+            nc.vector.tensor_copy(words[:], table[:].bitcast(U32).indirect(half_of(list_tile, half)))
+            return words
 
         k1_words = keep.tile([P, H], U32, name="k1_words", align_bytes=64)
-        w1 = keep.tile([P, H], U32, name="w1", align_bytes=64)
-        w1_scales = keep.tile([P, H], U8, name="w1_scales", align_bytes=64)
-        x_sel = [keep.tile([P, HALF], U32, name="x_sel%d" % half, tag="page%d" % (2 + half), align_bytes=64) for half in range(2)]
+        w1 = keep.tile([P, PACK, P], U32, name="w1", align_bytes=64)
+        first_scales = keep.tile([P, P], U8, name="first_scales", align_bytes=64)
+        other_scales = keep.tile([P, PACK - 1, P], U8, name="other_scales", align_bytes=64)
+        k1_rows = placed[:, 0:H].rearrange("p (m t) -> p t m", t=PACK)
+        nc.vector.tensor_copy(k1_words[:], d_word_tab[:].bitcast(U32).indirect(k1_list[:]))
+        nc.vector.tensor_copy(w1[:], k1_words[:].rearrange("p (m t) -> p t m", t=PACK))
+        w2 = [pick_half("w2_low", "w2_low", d_word_tab, k2_list, 0)]
+        tokens = [pick_half("tokens_low", "page2", x_word_tab, offs_list, 0)]
+        nc.vector.tensor_copy(first_scales[:], k1_rows[:, first, :])
+        tokens.append(pick_half("tokens_high", "page3", x_word_tab, offs_list, 1))
+        nc.vector.tensor_copy(other_scales[:], k1_rows[:, first + 1 :, :])
+        place_scale_rows(nc.sync, W2_ROW0, k2_bytes)
+        w2.append(pick_half("w2_high", "w2_high", d_word_tab, k2_list, 1))
 
-        def pick_tokens(half):
-            nc.vector.tensor_copy(
-                x_sel[half][:],
-                x_word_tab[:].bitcast(U32).indirect(offs_t[:, half * HALF // 16 : (half + 1) * HALF // 16]),
-            )
-
-        nc.vector.tensor_copy(k1_words[:], d_word_tab[:].bitcast(U32).indirect(k1_t[:]))
-        nc.vector.tensor_copy(
-            w1[:].rearrange("p (t m) -> p t m", t=PACK),
-            k1_words[:].rearrange("p (m t) -> p t m", t=PACK),
-        )
-        pick_tokens(0)
-        nc.vector.tensor_copy(
-            w1_scales[:].rearrange("p (t m) -> p t m", t=PACK),
-            placed[:, 0:H].rearrange("p (m t) -> p t m", t=PACK),
-        )
-        place_scale_rows(nc.sync, 4, k2_bytes)
-        pick_tokens(1)
-        w2 = keep.tile([P, H], U32, name="w2", tag="w2", align_bytes=64)
-        nc.vector.tensor_copy(w2[:], d_word_tab[:].bitcast(U32).indirect(k2_t[:]))
-
+        mem_planes = mem.rearrange("(p t) w -> p t w", t=PACK)
+        pages = {}
         for n, t in enumerate(PLANE_ORDER):
-            pages[t] = keep.tile([P, U], F32, name="page%d" % t, tag="page%d" % n, align_bytes=64)
-            nc.sync.dma_start(pages[t][:], mem_rows[:, t, :])
+            pages[t] = keep.tile([P, U], F32, name="page_plane%d" % t, tag="page%d" % n, align_bytes=64)
+            nc.sync.dma_start(pages[t][:], mem_planes[:, t, :])
 
-        def first_layer(t, h, halves):
-            acc = psum.tile([P, len(halves), HALF], F32, name="acc", tag="bank")
-            cols = slice(P * t, P * (t + 1))
+        def first_layer(t, halves, name, tag):
+            acc = psum.tile([P, len(halves), HALF], F32, name="acc_h", tag="bank")
             for i, half in enumerate(halves):
                 nc.tensor.matmul_mx(
                     out=acc[:, i, :],
-                    lhsT=w1[:, cols].bitcast(FP8X4),
-                    lhsT_scale=w1_scales[:, cols],
-                    rhs=x_sel[half][:].bitcast(FP8X4),
-                    rhs_scale=x_sel_scales[:, half * HALF : (half + 1) * HALF],
+                    lhsT=w1[:, t, :].bitcast(FP8X4),
+                    lhsT_scale=first_scales[:] if t == first else other_scales[:, t - first - 1, :],
+                    rhs=tokens[half][:].bitcast(FP8X4),
+                    rhs_scale=placed[:, H + half * HALF : H + (half + 1) * HALF],
                     start=True,
                     stop=True,
                 )
+            h = keep.tile([P, len(halves) * HALF], F32, name=name, tag=tag, align_bytes=64)
             nc.scalar.activation(h[:], acc[:].rearrange("p i s -> p (i s)"), RELU, scale=SIXTEENTH)
+            return h
 
-        h_first = [keep.tile([P, HALF], F32, name="h_first%d" % half) for half in range(2)]
-        for half in range(2):
-            first_layer(first, h_first[half], (half,))
-        hs = {}
-        for t in PLANE_ORDER[1:-1]:
-            hs[t] = keep.tile([P, S], F32, name="h%d" % t)
-            first_layer(t, hs[t], (0, 1))
+        h_first = [first_layer(first, (half,), "h_first%d" % half, "h_first%d" % half) for half in range(2)]
+        h_planes = {t: first_layer(t, (0, 1), "h%d" % t, "h%d" % t) for t in PLANE_ORDER[1:-1]}
 
-        n_chunks = U // CHUNK
-        z = [keep.tile([P, CHUNK, PACK], BF16, name="z%d" % c, align_bytes=64) for c in range(n_chunks)]
-        late = {c: keep.tile([P, 2, CHUNK], BF16, name="late%d" % c, align_bytes=64) for c in range(1, n_chunks)}
+        chunks = range(len(WIDTHS))
+        starts = [sum(WIDTHS[:c]) for c in chunks]
+        z = [keep.tile([P, WIDTHS[c], PACK], BF16, name="z%d" % c, align_bytes=64) for c in chunks]
+        pairs = {c: keep.tile([P, 2, WIDTHS[c]], BF16, name="pairs%d" % c, align_bytes=64) for c in chunks[DIRECT:]}
 
         def page_chunk(t, c):
-            return pages[t][:, c * CHUNK : (c + 1) * CHUNK]
+            return pages[t][:, starts[c] : starts[c] + WIDTHS[c]]
 
-        def weigh(t, chunks):
-            for c in chunks:
-                target = late[c][:, t - 2, :] if t >= 2 and c in late else z[c][:, :, t]
+        def weigh_on_scalar(t, some_chunks):
+            for c in some_chunks:
+                target = pairs[c][:, t, :] if c in pairs and t in (first, last) else z[c][:, :, t]
                 nc.scalar.activation(target, page_chunk(t, c), COPY, scale=gain[:, t : t + 1])
 
         for half in range(2):
-            offsets = slot_t[:, half * HALF // 16 : (half + 1) * HALF // 16]
-            nc.vector.tensor_copy(pages[first][:].indirect(offsets), h_first[half][:])
-        weigh(first, range(n_chunks))
-        hs[last] = keep.tile([P, S], F32, name="h_last", tag="page0", align_bytes=64)
-        first_layer(last, hs[last], (0, 1))
+            nc.vector.tensor_copy(pages[first][:].indirect(half_of(slot_list, half)), h_first[half][:])
+        weigh_on_scalar(first, chunks)
+        h_planes[last] = first_layer(last, (0, 1), "h_last", "page0")
         for t in PLANE_ORDER[1:-1]:
-            nc.vector.tensor_copy(pages[t][:].indirect(slot_t[:]), hs[t][:])
-            weigh(t, range(n_chunks))
-        nc.vector.tensor_copy(pages[last][:].indirect(slot_t[:]), hs[last][:])
-        nc.vector.tensor_scalar(z[0][:, :, last], page_chunk(last, 0), gain[:, last : last + 1], None, MULT)
-        weigh(last, range(1, n_chunks))
+            nc.vector.tensor_copy(pages[t][:].indirect(slot_list[:]), h_planes[t][:])
+            weigh_on_scalar(t, chunks)
+        nc.vector.tensor_copy(pages[last][:].indirect(slot_list[:]), h_planes[last][:])
+        for c in chunks[:DIRECT]:
+            nc.vector.tensor_scalar(z[c][:, :, last], page_chunk(last, c), gain[:, last : last + 1], None, MULT)
+        weigh_on_scalar(last, chunks[DIRECT:])
 
-        out_rows = out.rearrange("(m p) w -> p m w", p=P)
-        spans = ((0, 1), (1, 2), (2, 4))
-        codes, z_scales, home = {}, {}, {}
-        for c0, c1 in spans:
-            codes[c0] = keep.tile([P, (c1 - c0) * CHUNK], U32, name="codes%d" % c0, align_bytes=64)
-            z_scales[c0] = keep.tile([P, (c1 - c0) * CHUNK], U8, name="z_scales%d" % c0, align_bytes=64)
-            for c in range(c0, c1):
-                home[c] = (c0, slice((c - c0) * CHUNK, (c - c0 + 1) * CHUNK))
+        out_blocks = out.rearrange("(m p) w -> p m w", p=P)
 
-        def pair(c):
-            nc.vector.tensor_copy(z[c][:, :, 2:4], late[c][:].rearrange("p t w -> p w t"))
+        def lay_pairs(c):
+            nc.vector.tensor_copy(z[c][:, :, 0:2], pairs[c][:].rearrange("p t w -> p w t"))
 
-        def quantize(c):
-            c0, cols = home[c]
-            nc.vector.quantize_mx(codes[c0][:, cols].bitcast(FP8X4), z_scales[c0][:, cols], z[c][:].rearrange("p w t -> p (w t)"))
+        def quantise(span):
+            c0, width = span[0], sum(WIDTHS[c] for c in span)
+            codes = keep.tile([P, width], U32, name="codes%d" % c0, align_bytes=64)
+            scales = keep.tile([P, width], U8, name="scales%d" % c0, align_bytes=64)
+            for c in span:
+                cols = slice(starts[c] - starts[c0], starts[c] - starts[c0] + WIDTHS[c])
+                nc.vector.quantize_mx(codes[:, cols].bitcast(FP8X4), scales[:, cols], z[c][:].rearrange("p w t -> p (w t)"))
+            return codes, scales, slice(starts[c0], starts[c0] + width)
 
-        def second_layer(c0, c1, blocks, on_vector):
-            width = (c1 - c0) * CHUNK
-            acc = psum.tile([P, len(blocks), width], F32, name="acc2", tag="bank")
+        def second_layer(operand, blocks, on_vector):
+            codes, scales, cols = operand
+            width = cols.stop - cols.start
+            acc = psum.tile([P, len(blocks), width], F32, name="acc_out", tag="bank")
             for i, m in enumerate(blocks):
-                cols = slice(P * m, P * (m + 1))
+                half, local = divmod(m, BLOCKS_PER_HALF)
                 nc.tensor.matmul_mx(
                     out=acc[:, i, :],
-                    lhsT=w2[:, cols].bitcast(FP8X4),
-                    lhsT_scale=placed[4:P, cols],
-                    rhs=codes[c0][:].bitcast(FP8X4),
-                    rhs_scale=z_scales[c0][:],
+                    lhsT=w2[half][:, P * local : P * (local + 1)].bitcast(FP8X4),
+                    lhsT_scale=placed[W2_ROW0:P, P * m : P * (m + 1)],
+                    rhs=codes[:].bitcast(FP8X4),
+                    rhs_scale=scales[:],
                     start=True,
                     stop=True,
                 )
-            res = keep.tile([P, len(blocks), width], F32, name="res%d_%d" % (c0, blocks[0]))
+            result = keep.tile([P, len(blocks), width], F32, name="result%d_%d" % (cols.start, blocks[0]))
             if on_vector:
-                nc.vector.tensor_scalar(res[:], acc[:], SIXTEENTH, None, MULT)
+                nc.vector.tensor_scalar(result[:], acc[:], SIXTEENTH, None, MULT)
             else:
-                nc.scalar.activation(res[:], acc[:], COPY, scale=SIXTEENTH)
-            nc.sync.dma_start(out_rows[:, blocks[0] : blocks[-1] + 1, c0 * CHUNK : c1 * CHUNK], res[:])
+                nc.scalar.activation(result[:], acc[:], COPY, scale=SIXTEENTH)
+            nc.sync.dma_start(out_blocks[:, blocks[0] : blocks[-1] + 1, cols], result[:])
 
-        quantize(0)
+        middle, late, latest = chunks[DIRECT:]
+        operand = quantise(chunks[:DIRECT])
         for blocks in ((0,), (1,), (2, 3)):
-            second_layer(0, 1, blocks, False)
-        pair(1)
-        pair(2)
-        quantize(1)
+            second_layer(operand, blocks, False)
+        lay_pairs(middle)
+        lay_pairs(late)
+        operand = quantise((middle,))
         for blocks in ((0, 1), (2, 3)):
-            second_layer(1, 2, blocks, False)
-        pair(3)
-        quantize(2)
-        quantize(3)
+            second_layer(operand, blocks, False)
+        lay_pairs(latest)
+        operand = quantise((late, latest))
         for m in range(H // P):
-            second_layer(2, 4, (m,), m % 2 == 1)
+            second_layer(operand, (m,), m % 2 == 1)

from contextlib import ExitStack

import concourse.mybir as mybir

K, T, S, U, G, H = 512, 2048, 512, 1024, 2048, 512
FLOPS = 2 * K * H * S + 2 * K * H * U

F32 = mybir.dt.float32
BF16 = mybir.dt.bfloat16
I32 = mybir.dt.int32
U32 = mybir.dt.uint32
U16 = mybir.dt.uint16
U8 = mybir.dt.uint8
FP8X4 = mybir.dt.float8_e4m3fn_x4
RELU = mybir.ActivationFunctionType.Relu
COPY = mybir.ActivationFunctionType.Copy
MULT = mybir.AluOpType.mult

P = 128
PACK = 4
GROUP = 16
BLOCK_P = 8
QUAD = 32
W2_ROW0 = 4
HALF = 256
WORD_BYTES = 4
BANKS = 8
SIXTEENTH = 0.0625

PLANE_ORDER = (0, 2, 3, 1)
WIDTHS = (128, 128, 256, 256, 256)
DIRECT = 2
BLOCKS_PER_HALF = HALF // P


def tile_picked_pqscat_relu_p_kernel(tc, x_words, x_scales, d_words, d_scales, mem, gs, offs, k1, slot, k2, out):
    nc = tc.nc
    first, last = PLANE_ORDER[0], PLANE_ORDER[-1]
    with ExitStack() as ctx:
        lists = ctx.enter_context(tc.tile_pool(name="lists", bufs=1))
        keep = ctx.enter_context(tc.tile_pool(name="keep", bufs=1))
        psum = ctx.enter_context(tc.psum_pool(name="psum", bufs=BANKS))

        k1_list = lists.tile([P, H // GROUP], U16, name="k1_list")
        offs_list = lists.tile([P, S // GROUP], U16, name="offs_list")
        k2_list = lists.tile([P, H // GROUP], U16, name="k2_list")
        slot_list = lists.tile([P, S // GROUP], U16, name="slot_list")
        d_scale_tab = keep.tile([P, G], U8, name="d_scale_tab", tag="page0", align_bytes=64)
        x_scale_tab = keep.tile([P, T], U8, name="x_scale_tab", align_bytes=64)
        d_word_tab = keep.tile([P, G], I32, name="d_word_tab", tag="page1", align_bytes=64)
        x_word_tab = keep.tile([P, T], I32, name="x_word_tab", tag="w2_high", align_bytes=64)
        placed = keep.tile([P, H + S], U8, name="placed", align_bytes=64)
        gain = keep.tile([P, PACK], F32, name="gain")

        def half_of(list_tile, half):
            return list_tile[:, half * HALF // GROUP : (half + 1) * HALF // GROUP]

        nc.vector.memset(x_scale_tab[:].bitcast(I32), 0)
        nc.vector.memset(placed[:].bitcast(I32), 0)
        nc.sync.dma_start(k1_list[:], k1)
        nc.sync.dma_start(
            d_scale_tab[:].bitcast(I32),
            d_scales[0].bitcast(I32).unsqueeze(1).to_broadcast([P // BLOCK_P, BLOCK_P, G // WORD_BYTES]),
        )
        nc.sync.dma_start(offs_list[:], offs)
        nc.sync.dma_start(k2_list[:], k2)
        nc.sync.dma_start(slot_list[:], slot)
        nc.sync.dma_start(x_scale_tab[0:P:BLOCK_P, :].bitcast(I32), x_scales[0].bitcast(I32))
        nc.sync.dma_start(d_word_tab[:], d_words[0].rearrange("p c r -> p (c r)").bitcast(I32))
        nc.sync.dma_start(x_word_tab[:], x_words[0].rearrange("p c r -> p (c r)").bitcast(I32))
        nc.sync.dma_start(gain[:], gs.rearrange("(p t) o -> p (t o)", t=PACK))

        def place_scale_rows(queue, row0, picked):
            width = picked.shape[1]
            for q in range(P // QUAD):
                target = placed[QUAD * q + row0 : QUAD * q + row0 + QUAD // BLOCK_P, 0:width]
                queue.dma_start(target.bitcast(I32), picked[QUAD * q : QUAD * (q + 1) : BLOCK_P, :].bitcast(I32))

        first_bytes = keep.tile([P, H + S], U8, name="first_bytes", tag="page3", align_bytes=64)
        k2_bytes = keep.tile([P, H], U8, name="k2_bytes", align_bytes=64)
        nc.vector.tensor_copy(first_bytes[:, 0:H], d_scale_tab[:].indirect(k1_list[:]))
        nc.vector.tensor_copy(first_bytes[:, H:], x_scale_tab[:].indirect(offs_list[:]))
        place_scale_rows(nc.scalar, 0, first_bytes)
        nc.vector.tensor_copy(k2_bytes[:], d_scale_tab[:].indirect(k2_list[:]))

        def pick_half(name, tag, table, list_tile, half):
            words = keep.tile([P, HALF], U32, name=name, tag=tag, align_bytes=64)
            nc.vector.tensor_copy(words[:], table[:].bitcast(U32).indirect(half_of(list_tile, half)))
            return words

        k1_words = keep.tile([P, H], U32, name="k1_words", align_bytes=64)
        w1 = keep.tile([P, PACK, P], U32, name="w1", align_bytes=64)
        first_scales = keep.tile([P, P], U8, name="first_scales", align_bytes=64)
        other_scales = keep.tile([P, PACK - 1, P], U8, name="other_scales", align_bytes=64)
        k1_rows = placed[:, 0:H].rearrange("p (m t) -> p t m", t=PACK)
        nc.vector.tensor_copy(k1_words[:], d_word_tab[:].bitcast(U32).indirect(k1_list[:]))
        nc.vector.tensor_copy(w1[:], k1_words[:].rearrange("p (m t) -> p t m", t=PACK))
        w2 = [pick_half("w2_low", "w2_low", d_word_tab, k2_list, 0)]
        tokens = [pick_half("tokens_low", "page2", x_word_tab, offs_list, 0)]
        nc.vector.tensor_copy(first_scales[:], k1_rows[:, first, :])
        tokens.append(pick_half("tokens_high", "page3", x_word_tab, offs_list, 1))
        nc.vector.tensor_copy(other_scales[:], k1_rows[:, first + 1 :, :])
        place_scale_rows(nc.sync, W2_ROW0, k2_bytes)
        w2.append(pick_half("w2_high", "w2_high", d_word_tab, k2_list, 1))

        mem_planes = mem.rearrange("(p t) w -> p t w", t=PACK)
        pages = {}
        for n, t in enumerate(PLANE_ORDER):
            pages[t] = keep.tile([P, U], F32, name="page_plane%d" % t, tag="page%d" % n, align_bytes=64)
            nc.sync.dma_start(pages[t][:], mem_planes[:, t, :])

        def first_layer(t, halves, name, tag):
            acc = psum.tile([P, len(halves), HALF], F32, name="acc_h", tag="bank")
            for i, half in enumerate(halves):
                nc.tensor.matmul_mx(
                    out=acc[:, i, :],
                    lhsT=w1[:, t, :].bitcast(FP8X4),
                    lhsT_scale=first_scales[:] if t == first else other_scales[:, t - first - 1, :],
                    rhs=tokens[half][:].bitcast(FP8X4),
                    rhs_scale=placed[:, H + half * HALF : H + (half + 1) * HALF],
                    start=True,
                    stop=True,
                )
            h = keep.tile([P, len(halves) * HALF], F32, name=name, tag=tag, align_bytes=64)
            nc.scalar.activation(h[:], acc[:].rearrange("p i s -> p (i s)"), RELU, scale=SIXTEENTH)
            return h

        h_first = [first_layer(first, (half,), "h_first%d" % half, "h_first%d" % half) for half in range(2)]
        h_planes = {t: first_layer(t, (0, 1), "h%d" % t, "h%d" % t) for t in PLANE_ORDER[1:-1]}

        chunks = range(len(WIDTHS))
        starts = [sum(WIDTHS[:c]) for c in chunks]
        z = [keep.tile([P, WIDTHS[c], PACK], BF16, name="z%d" % c, align_bytes=64) for c in chunks]
        pairs = {c: keep.tile([P, 2, WIDTHS[c]], BF16, name="pairs%d" % c, align_bytes=64) for c in chunks[DIRECT:]}

        def page_chunk(t, c):
            return pages[t][:, starts[c] : starts[c] + WIDTHS[c]]

        def weigh_on_scalar(t, some_chunks):
            for c in some_chunks:
                target = pairs[c][:, t, :] if c in pairs and t in (first, last) else z[c][:, :, t]
                nc.scalar.activation(target, page_chunk(t, c), COPY, scale=gain[:, t : t + 1])

        for half in range(2):
            nc.vector.tensor_copy(pages[first][:].indirect(half_of(slot_list, half)), h_first[half][:])
        weigh_on_scalar(first, chunks)
        h_planes[last] = first_layer(last, (0, 1), "h_last", "page0")
        for t in PLANE_ORDER[1:-1]:
            nc.vector.tensor_copy(pages[t][:].indirect(slot_list[:]), h_planes[t][:])
            weigh_on_scalar(t, chunks)
        nc.vector.tensor_copy(pages[last][:].indirect(slot_list[:]), h_planes[last][:])
        for c in chunks[:DIRECT]:
            nc.vector.tensor_scalar(z[c][:, :, last], page_chunk(last, c), gain[:, last : last + 1], None, MULT)
        weigh_on_scalar(last, chunks[DIRECT:])

        out_blocks = out.rearrange("(m p) w -> p m w", p=P)

        def lay_pairs(c):
            nc.vector.tensor_copy(z[c][:, :, 0:2], pairs[c][:].rearrange("p t w -> p w t"))

        def quantise(span):
            c0, width = span[0], sum(WIDTHS[c] for c in span)
            codes = keep.tile([P, width], U32, name="codes%d" % c0, align_bytes=64)
            scales = keep.tile([P, width], U8, name="scales%d" % c0, align_bytes=64)
            for c in span:
                cols = slice(starts[c] - starts[c0], starts[c] - starts[c0] + WIDTHS[c])
                nc.vector.quantize_mx(codes[:, cols].bitcast(FP8X4), scales[:, cols], z[c][:].rearrange("p w t -> p (w t)"))
            return codes, scales, slice(starts[c0], starts[c0] + width)

        def second_layer(operand, blocks, on_vector):
            codes, scales, cols = operand
            width = cols.stop - cols.start
            acc = psum.tile([P, len(blocks), width], F32, name="acc_out", tag="bank")
            for i, m in enumerate(blocks):
                half, local = divmod(m, BLOCKS_PER_HALF)
                nc.tensor.matmul_mx(
                    out=acc[:, i, :],
                    lhsT=w2[half][:, P * local : P * (local + 1)].bitcast(FP8X4),
                    lhsT_scale=placed[W2_ROW0:P, P * m : P * (m + 1)],
                    rhs=codes[:].bitcast(FP8X4),
                    rhs_scale=scales[:],
                    start=True,
                    stop=True,
                )
            result = keep.tile([P, len(blocks), width], F32, name="result%d_%d" % (cols.start, blocks[0]))
            if on_vector:
                nc.vector.tensor_scalar(result[:], acc[:], SIXTEENTH, None, MULT)
            else:
                nc.scalar.activation(result[:], acc[:], COPY, scale=SIXTEENTH)
            nc.sync.dma_start(out_blocks[:, blocks[0] : blocks[-1] + 1, cols], result[:])

        middle, late, latest = chunks[DIRECT:]
        operand = quantise(chunks[:DIRECT])
        for blocks in ((0,), (1,), (2, 3)):
            second_layer(operand, blocks, False)
        lay_pairs(middle)
        lay_pairs(late)
        operand = quantise((middle,))
        for blocks in ((0, 1), (2, 3)):
            second_layer(operand, blocks, False)
        lay_pairs(latest)
        operand = quantise((late, latest))
        for m in range(H // P):
            second_layer(operand, (m,), m % 2 == 1)
